import numpy as np, ml_dtypes
CORES = [13,21,141,149]
N = 4
import mx_ref
NC = 512
BF = ml_dtypes.bfloat16
def cut(t, i, w=512):
    return t[:, w * i:w * i + w]
def term(a, B):
    return np.stack([np.maximum(mx_ref.matmul(mx_ref.quantize(cut(a, i)), B), 0) for i in range(4)], axis=2).reshape(128, -1)
def setup_inputs(rng):
    def f(*shape):
        return mx_ref.flush((rng.standard_normal(shape, dtype=np.float32) * np.exp2(rng.integers(-2, 3, shape[:-1] + (1,)))).astype(BF))
    return {"a": f(N, 128, 4 * 512), "b": f(N, 128, 4 * NC)}
def setup_inputs_blocks(rng):
    d = setup_inputs(rng)
    for k in ("a", "b"): d[k] = mx_ref.spread(d[k], rng, 2)
    return d
def setup_inputs_wide(rng):
    d = setup_inputs(rng)
    for k in ("a", "b"): d[k] = mx_ref.flush((d[k].astype(np.float32) * np.exp2(rng.integers(-4, 5, (N, 1, 1))).astype(np.float32)).astype(BF))
    return d
def setup_inputs_lossless(rng):
    a = np.zeros((N, 128, 4 * 128, 4), np.float32)
    for r in range(N):
        k = rng.integers(0, 512, size=4 * 128)
        a[r, k // 4, np.arange(4 * 128), k % 4] = 1.0
    size = np.repeat(2.0 ** rng.integers(-4, 5, size=(1, 1, (4 * NC) // 4)), 4, axis=2)
    b = (rng.random((N, 128, 4 * NC)) < 0.8) * size
    return {"a": a.reshape(N, 128, 4 * 512).astype(BF), "b": b.astype(np.float32).astype(BF)}
def reference(a, b):
    Bq = [mx_ref.quantize(b[c]) for c in range(N)]
    y = np.zeros((N, 128, 4 * NC), np.float32)
    for c in range(N):
        y[c] = mx_ref.total([term(a[r], Bq[c]) for r in range(N)])
    return {"y": y}

import numpy as np
from concourse.bass import DstId, RemoteDMATransfer
from concourse.mybir import dt, AluOpType, ActivationFunctionType

F32, BF16, CODE, U8 = "float32", "bfloat16", "float8_e4m3fn_x4", "uint8"
W = 512
H = W // 2
M = 128

SCRATCH = {
    "ta": ("sbuf", [128, 4 * W], BF16), "tb": ("sbuf", [128, 4 * W], BF16),
    "cO": ("sbuf", [128, W], CODE), "sO": ("sbuf", [128, W], U8),
    "cQ": ("sbuf", [128, W], CODE), "sQ": ("sbuf", [128, W], U8),
    "cP": ("sbuf", [128, W], CODE), "sP": ("sbuf", [128, W], U8),
    "cA": ("sbuf", [128, W], CODE), "sA": ("sbuf", [128, W], U8),
    "cB": ("sbuf", [128, W], CODE), "sB": ("sbuf", [128, W], U8),
    "cR": ("sbuf", [128, H], CODE), "sR": ("sbuf", [128, H], U8),
    "zO": ("sbuf", [128, 4 * W], F32), "zP": ("sbuf", [128, 4 * W], F32),
    "zA": ("sbuf", [128, 4 * W], F32), "zB": ("sbuf", [128, 4 * W], F32),
    "s1": ("sbuf", [128, 4 * W], F32), "s2": ("sbuf", [128, 4 * W], F32),
    "yt": ("sbuf", [128, 4 * W], F32),
    "ps": ("psum", [128, 8 * 512], F32),
}
SEMAPHORES = ["la0", "la1", "lb", "qa", "qb", "pe", "sc", "ve", "sent", "stored", "rS", "rC", "arrP", "arrA0", "arrA1", "arrB0", "arrB1"]


def spread_mask(mask, parts):
    bits = [1 << k for k in range(16) if mask >> k & 1]
    return [sum(bits[p::parts]) for p in range(parts)]


def relays(rc, far, topo):
    chip = [c for c in range(256) if topo.host(c) == topo.host(rc) and topo.chip(c) == topo.chip(rc) and c != rc]
    ok = [c for c in chip if all(topo.may_write(c, f) for f in far)]
    mine = [c for c in ok if topo.die(c) == topo.die(rc)]
    other = [c for c in ok if topo.die(c) != topo.die(rc)]
    return [mine[0], other[0]]


def peers(rc, cores, topo):
    p = [c for c in cores if topo.same_plane(c, rc)][0]
    far = [c for c in cores if c not in (rc, p)]
    a = [c for c in far if topo.host(c) == topo.host(rc)][0]
    b = [c for c in far if c != a][0]
    return p, a, b


def copy_to(dst, src, topo, out, in_, sem, mask):
    rid, pid = topo.addr(dst, src)
    return RemoteDMATransfer(dst_ids=[DstId(rid=rid, pnc=pid)], dma_engine_mask=mask, remote_sem=sem, srcs=[in_], dsts=[out])


def half(t, k):
    return t[:, H * k:H * k + H]


def bytes_of(view):
    return view.bitcast(dt.uint8)


def relay_program(g, core, T, topo, k, a, b):
    sem = T.sem
    full = topo.mask(core, a) & topo.mask(core, b)
    ma, mb = spread_mask(full, 2)
    n = bin(ma).count("1")
    g.wait_ge(sem.rS, 8)
    g.remote_dma_fused([copy_to(a, core, topo, half(T.sA, k), T.sR[:], sem["arrA%d" % k], ma),
                        copy_to(b, core, topo, half(T.sB, k), T.sR[:], sem["arrB%d" % k], mb)], local_sem=sem.sent)
    g.wait_ge(sem.rC, 8)
    for d, buf, s in ((a, T.cA, sem["arrA%d" % k]), (b, T.cB, sem["arrB%d" % k])):
        rid, pid = topo.addr(d, core)
        g.remote_dma(bytes_of(half(buf, k)), bytes_of(T.cR[:]), s, sem.sent, pid, rid, full)
    g.wait_ge(sem.sent, 2 * n + 2 * 2 * n)


def rank_program(g, core, T, topo):
    sem = T.sem
    rank = T.rank_of(core)
    if rank is None:
        for rc in T.cores:
            p, a, b = peers(rc, T.cores, topo)
            rel = relays(rc, (a, b), topo)
            if core in rel:
                relay_program(g, core, T, topo, rel.index(core), a, b)
        return
    p, a, b = peers(core, T.cores, topo)
    rel = relays(core, (a, b), topo)
    add, relu = AluOpType.add, ActivationFunctionType.Relu

    g.sync.dma_start(T.ta[:, 0:4 * H], T.a[:, 0:4 * H]).then_inc(sem.la0, 16)
    g.scalar.dma_start(T.ta[:, 4 * H:8 * H], T.a[:, 4 * H:8 * H]).then_inc(sem.la1, 16)
    g.sync.dma_start(T.tb[:], T.b[:]).then_inc(sem.lb, 16)

    for k in range(2):
        g.vector.wait_ge(sem["la%d" % k], 16)
        g.vector.quantize_mx(half(T.cO, k), half(T.sO, k), T.ta[:, 4 * H * k:4 * H * k + 4 * H]).then_inc(sem.qa, 1)
    g.vector.wait_ge(sem.lb, 16)
    g.vector.quantize_mx(T.cQ[:], T.sQ[:], T.tb[:]).then_inc(sem.qb, 1)

    g.wait_ge(sem.qa, 2)
    masks = spread_mask(topo.mask(core, rel[0]) & topo.mask(core, rel[1]), 2)
    g.remote_dma_fused([copy_to(rel[k], core, topo, T.sR[:], half(T.sO, k), sem.rS, masks[k]) for k in range(2)], local_sem=sem.sent)
    g.remote_dma_fused([copy_to(rel[k], core, topo, bytes_of(T.cR[:]), bytes_of(half(T.cO, k)), sem.rC, masks[k]) for k in range(2)], local_sem=sem.sent)
    rid, pid = topo.addr(p, core)
    mp = topo.mask(core, p)
    g.remote_dma(T.sP[:], T.sO[:], sem.arrP, sem.sent, pid, rid, mp)
    g.remote_dma(bytes_of(T.cP[:]), bytes_of(T.cO[:]), sem.arrP, sem.sent, pid, rid, mp)

    units = [(s, i, 0, W) for s in "OPA" for i in range(4)] + [("B", i, j, H) for j in (0, H) for i in range(4)]
    need = {"P": {0: [("arrP", 16)]}, "A": {0: [("arrA0", 12)], 2: [("arrA1", 12)]}, "B": {0: [("arrB0", 12)], 2: [("arrB1", 12)]}}

    g.tensor.wait_ge(sem.qa, 2)
    g.tensor.wait_ge(sem.qb, 1)
    for u, (s, i, j, n) in enumerate(units):
        if j == 0:
            for name, v in need.get(s, {}).get(i, []):
                g.tensor.wait_ge(sem[name], v)
        if u >= 8:
            g.tensor.wait_ge(sem.sc, u - 7)
        bank = 512 * (u % 8)
        g.tensor.matmul_mx(T.ps[:, bank:bank + n], T["c" + s][:, M * i:M * i + M], T["s" + s][:, M * i:M * i + M],
                           T.cQ[:, j:j + n], T.sQ[:, j:j + n], True, True).then_inc(sem.pe, 1)

    for u, (s, i, j, n) in enumerate(units):
        bank = 512 * (u % 8)
        g.scalar.wait_ge(sem.pe, u + 1)
        g.scalar.activation(T["z" + s][:, W * i + j:W * i + j + n], T.ps[:, bank:bank + n], relu).then_inc(sem.sc, 1)

    v = 0
    for u, (s, i, j, n) in enumerate(units):
        if s == "O":
            continue
        c = slice(W * i + j, W * i + j + n)
        g.vector.wait_ge(sem.sc, u + 1)
        if s == "A":
            g.vector.wait_ge(sem.ve, i + 1)
        if s == "B":
            g.vector.wait_ge(sem.ve, 4 + i + 1)
        if s == "P":
            g.vector.tensor_tensor(T.s1[:, c], T.zO[:, c], T.zP[:, c], add).then_inc(sem.ve, 1)
        elif s == "A":
            g.vector.tensor_tensor(T.s2[:, c], T.s1[:, c], T.zA[:, c], add).then_inc(sem.ve, 1)
        else:
            g.vector.tensor_tensor(T.yt[:, 4 * j + i:4 * (j + n):4], T.s2[:, c], T.zB[:, c], add).then_inc(sem.ve, 1)

    for k in range(2):
        g.sync.wait_ge(sem.ve, 12 + 4 * k)
        g.sync.dma_start(T.y[:, 4 * H * k:4 * H * k + 4 * H], T.yt[:, 4 * H * k:4 * H * k + 4 * H]).then_inc(sem.stored, 16)
    g.sync.wait_ge(sem.stored, 32)
    g.wait_ge(sem.sent, 48)
